import numpy as np
import ml_dtypes


def mxq(x, axis, fmt="e4m3"):
    dtype, down = {"e4m3": (ml_dtypes.float8_e4m3fn, 7), "e5m2": (ml_dtypes.float8_e5m2, 14)}[fmt]
    v = np.moveaxis(np.asarray(x, np.float32).astype(ml_dtypes.bfloat16).astype(np.float64), axis, -1)
    blocks = v.reshape(v.shape[:-1] + (-1, 32))
    amax = np.abs(blocks).max(-1, keepdims=True)
    byte = np.maximum(np.where(amax > 0, np.frexp(amax)[1] - 1 + 127, 0) - down, 1)
    scale = np.exp2(byte - 127.0)
    codes = (blocks / scale).astype(np.float32).astype(dtype).astype(np.float64)
    return np.moveaxis((codes * scale).reshape(v.shape), -1, axis)


WIDE = False


def mx_kscale(k):
    if not WIDE:
        return np.ones(k)
    levels = np.array([10, -10, 5, -5, 0])
    if k % 512:
        return np.exp2(np.random.permutation(np.resize(levels, k // 32))).repeat(32)
    a = np.empty((k // 512, 16))
    for p in range(k // 512):
        a[p, :8] = np.random.permutation(np.resize(levels, 8))
        for g in range(8):
            far = levels[np.abs(levels - a[p, g]) >= 10]
            a[p, g + 8] = far[np.random.randint(len(far))]
    return np.exp2(a.ravel()).repeat(32)


def f64(x):
    return np.asarray(x).astype(np.float64)


def striped(idx):
    return np.tile(idx.reshape(-1, 16).T, (8, 1)).astype(np.uint16)


def unstriped(offs):
    return offs[:16].T.reshape(-1).astype(np.int64)


E2M1 = np.array([0.0, 0.5, 1.0, 1.5, 2.0, 3.0, 4.0, 6.0, -0.0, -0.5, -1.0, -1.5, -2.0, -3.0, -4.0, -6.0])


def pack_fp4(w):
    k, n = w.shape
    w = f64(np.asarray(w, np.float32).astype(ml_dtypes.bfloat16)).reshape(k // 32, 32, n)
    amax = np.abs(w).max(1)
    mant, ex = np.frexp(amax / 6.0)
    byte = np.clip(np.where(amax > 0, np.where(mant > 0.5, ex, ex - 1) + 127, 1), 1, 254)
    scaled = (w * np.exp2(127.0 - byte)[:, None, :]).reshape(k, n).astype(np.float32)
    c = np.ascontiguousarray(scaled.reshape(k // 512, 128, 4, n).transpose(0, 1, 3, 2)).astype(ml_dtypes.float4_e2m1fn).view(np.uint8) & 0xF
    words = (c[..., 0::2] | (c[..., 1::2] << 4)).reshape(k // 512, 128, 2 * n)
    return np.ascontiguousarray(words), np.ascontiguousarray(byte.astype(np.uint8).reshape(k // 512, 16, n))


def unpack_fp4(words, scales):
    g, _, n = scales.shape
    words = np.ascontiguousarray(words).reshape(g, 128, n, 2)
    nib = np.empty((g, 128, n, 4), np.uint8)
    nib[..., 0::2] = words & 0xF
    nib[..., 1::2] = words >> 4
    vals = E2M1[nib] * np.repeat(np.exp2(scales.astype(np.float64) - 127.0), 8, axis=1)[..., None]
    return vals.transpose(0, 1, 3, 2).reshape(g * 512, n)


K, T, N, U = 512, 1024, 128, 2048


def setup_inputs():
    n = np.random.standard_normal
    s = mx_kscale(K)[:, None]
    packed_xT = pack_fp4(n((K, T)) * s)
    return {
        "x_words": packed_xT[0],
        "x_scales": packed_xT[1],
        "mem": n((N, U)).astype(np.float32),
        "w1": (n((K, N)) / np.sqrt(K) / s).astype(np.float32),
        "slot": striped(np.random.permutation(U)[:T]),
    }


def reference(x_words, x_scales, mem, w1, slot):
    xq = unpack_fp4(x_words, x_scales)
    y = np.tanh(mxq(f64(w1), 0, "e4m3").T @ xq)
    out = f64(mem).copy()
    out[:, unstriped(slot)] = y
    return out

@@ -1,0 +1,100 @@
+from contextlib import ExitStack
+
+import concourse.mybir as mybir
+
+K, T, M, U = 512, 1024, 128, 2048
+FLOPS = 2 * K * M * T
+
+F32 = mybir.dt.float32
+BF16 = mybir.dt.bfloat16
+I32 = mybir.dt.int32
+U32 = mybir.dt.uint32
+U16 = mybir.dt.uint16
+U8 = mybir.dt.uint8
+FP8X4 = mybir.dt.float8_e4m3fn_x4
+FP4X4 = mybir.dt.float4_e2m1fn_x4
+TANH = mybir.ActivationFunctionType.Tanh
+
+P = 128
+PACK = 4
+LOADS = ((0, 256), (256, 1024))
+PASSES = ((0, 256), (256, 512), (512, 768), (768, 1024))
+SCATTERS = (256, 1024)
+HALVES = ((0, 64), (64, 128))
+STORES = ((0, 2048),)
+
+
+def tile_picked_wkvput_tanh_l_kernel(tc, x_words, x_scales, mem, w1, slot, out):
+    nc = tc.nc
+    with ExitStack() as ctx:
+        keep = ctx.enter_context(tc.tile_pool(name="keep", bufs=1))
+        psum = ctx.enter_context(tc.psum_pool(name="psum", bufs=1))
+
+        offsets = keep.tile([P, T // 16], U16)
+        w_raw = keep.tile([P, PACK, M], F32)
+        x_tiles = [keep.tile([P, 2 * (hi - lo)], U8, align_bytes=64, name=f"x{lo}") for lo, hi in LOADS]
+        x_plane = keep.tile([P, T], U8, align_bytes=64)
+        window = keep.tile([P, U], F32)
+        warm_in = keep.tile([P, 1], F32)
+        warm_out = keep.tile([P, 1], F32)
+
+        def load_scales(queue, q):
+            queue.dma_start(
+                out=x_plane[32 * q : 32 * q + 4, :].bitcast(I32),
+                in_=x_scales[0, 4 * q : 4 * q + 4, :].bitcast(I32),
+            )
+
+        def load_words(queue, i):
+            lo, hi = LOADS[i]
+            queue.dma_start(out=x_tiles[i][:], in_=x_words[0, :, 2 * lo : 2 * hi])
+
+        nc.sync.dma_start(out=w_raw[:], in_=w1.rearrange("(p j) m -> p j m", j=PACK))
+        load_scales(nc.scalar, 0)
+        load_scales(nc.scalar, 1)
+        load_words(nc.sync, 0)
+        load_scales(nc.sync, 2)
+        load_scales(nc.sync, 3)
+        nc.sync.dma_start(out=window[:], in_=mem)
+        nc.sync.dma_start(offsets[:], slot)
+        load_words(nc.sync, 1)
+
+        nc.vector.memset(warm_in[:], 0.0)
+        nc.scalar.activation(warm_out[:], warm_in[:], TANH)
+
+        w_grouped = keep.tile([P, M, PACK], BF16, align_bytes=64)
+        w_codes = keep.tile([P, M], U32, align_bytes=64)
+        w_plane = keep.tile([P, M], U8, align_bytes=64)
+        for lo, hi in HALVES:
+            nc.vector.tensor_copy(
+                out=w_grouped[:, lo:hi, :].rearrange("p (c i) j -> p c j i", i=4),
+                in_=w_raw[:, :, lo:hi].rearrange("p j (c i) -> p c j i", i=4),
+            )
+        for lo, hi in HALVES:
+            nc.vector.quantize_mx(
+                out=w_codes[:, lo:hi].bitcast(FP8X4),
+                scales=w_plane[:, lo:hi],
+                in_=w_grouped[:, lo:hi, :].rearrange("p m j -> p (m j)"),
+            )
+
+        y = keep.tile([P, T], F32)
+        done = 0
+        for lo, hi in PASSES:
+            tile, base = [(t, a) for t, (a, b) in zip(x_tiles, LOADS) if a <= lo and hi <= b][0]
+            acc = psum.tile([P, hi - lo], F32, name=f"acc{lo}")
+            nc.tensor.matmul_mx(
+                out=acc[:],
+                lhsT=w_codes[:].bitcast(FP8X4),
+                lhsT_scale=w_plane[:],
+                rhs=tile[:, 2 * (lo - base) : 2 * (hi - base)].bitcast(FP4X4),
+                rhs_scale=x_plane[:, lo:hi],
+                start=True,
+                stop=True,
+            )
+            nc.scalar.activation(y[:, lo:hi], acc[:], TANH)
+            if hi in SCATTERS:
+                nc.vector.tensor_copy(window[:].indirect(offsets[:, done // 16 : hi // 16]), y[:, done:hi])
+                done = hi
+
+        for s, (lo, hi) in enumerate(STORES):
+            queue = nc.sync if s % 2 == 0 else nc.scalar
+            queue.dma_start(out=out[:, lo:hi], in_=window[:, lo:hi])

@@ -17,9 +17,9 @@ TANH = mybir.ActivationFunctionType.Tanh
 
 P = 128
 PACK = 4
-LOADS = ((0, 256), (256, 1024))
-PASSES = ((0, 256), (256, 512), (512, 768), (768, 1024))
-SCATTERS = (256, 1024)
+LOADS = ((0, 384), (384, 1024))
+PASSES = ((0, 256), (256, 384), (384, 640), (640, 896), (896, 1024))
+SCATTERS = (384, 1024)
 HALVES = ((0, 64), (64, 128))
 STORES = ((0, 2048),)
 
@@ -33,15 +33,16 @@ def tile_picked_wkvput_tanh_l_kernel(tc, x_words, x_scales, mem, w1, slot, out):
         offsets = keep.tile([P, T // 16], U16)
         w_raw = keep.tile([P, PACK, M], F32)
         x_tiles = [keep.tile([P, 2 * (hi - lo)], U8, align_bytes=64, name=f"x{lo}") for lo, hi in LOADS]
-        x_plane = keep.tile([P, T], U8, align_bytes=64)
+        planes = [keep.tile([P, hi - lo], U8, align_bytes=64, name=f"plane{lo}") for lo, hi in LOADS]
         window = keep.tile([P, U], F32)
         warm_in = keep.tile([P, 1], F32)
         warm_out = keep.tile([P, 1], F32)
 
-        def load_scales(queue, q):
+        def load_scales(queue, i, q):
+            lo, hi = LOADS[i]
             queue.dma_start(
-                out=x_plane[32 * q : 32 * q + 4, :].bitcast(I32),
-                in_=x_scales[0, 4 * q : 4 * q + 4, :].bitcast(I32),
+                out=planes[i][32 * q : 32 * q + 4, :].bitcast(I32),
+                in_=x_scales[0, 4 * q : 4 * q + 4, lo:hi].bitcast(I32),
             )
 
         def load_words(queue, i):
@@ -49,14 +50,16 @@ def tile_picked_wkvput_tanh_l_kernel(tc, x_words, x_scales, mem, w1, slot, out):
             queue.dma_start(out=x_tiles[i][:], in_=x_words[0, :, 2 * lo : 2 * hi])
 
         nc.sync.dma_start(out=w_raw[:], in_=w1.rearrange("(p j) m -> p j m", j=PACK))
-        load_scales(nc.scalar, 0)
-        load_scales(nc.scalar, 1)
+        load_scales(nc.scalar, 0, 0)
+        load_scales(nc.scalar, 0, 1)
         load_words(nc.sync, 0)
-        load_scales(nc.sync, 2)
-        load_scales(nc.sync, 3)
+        load_scales(nc.sync, 0, 2)
+        load_scales(nc.sync, 0, 3)
         nc.sync.dma_start(out=window[:], in_=mem)
         nc.sync.dma_start(offsets[:], slot)
         load_words(nc.sync, 1)
+        for q in range(4):
+            load_scales(nc.sync, 1, q)
 
         nc.vector.memset(warm_in[:], 0.0)
         nc.scalar.activation(warm_out[:], warm_in[:], TANH)
@@ -79,14 +82,14 @@ def tile_picked_wkvput_tanh_l_kernel(tc, x_words, x_scales, mem, w1, slot, out):
         y = keep.tile([P, T], F32)
         done = 0
         for lo, hi in PASSES:
-            tile, base = [(t, a) for t, (a, b) in zip(x_tiles, LOADS) if a <= lo and hi <= b][0]
+            tile, plane, base = [(t, s, a) for t, s, (a, b) in zip(x_tiles, planes, LOADS) if a <= lo and hi <= b][0]
             acc = psum.tile([P, hi - lo], F32, name=f"acc{lo}")
             nc.tensor.matmul_mx(
                 out=acc[:],
                 lhsT=w_codes[:].bitcast(FP8X4),
                 lhsT_scale=w_plane[:],
                 rhs=tile[:, 2 * (lo - base) : 2 * (hi - base)].bitcast(FP4X4),
-                rhs_scale=x_plane[:, lo:hi],
+                rhs_scale=plane[:, lo - base : hi - base],
                 start=True,
                 stop=True,
             )

@@ -35,14 +35,12 @@ def tile_picked_wkvput_tanh_l_kernel(tc, x_words, x_scales, mem, w1, slot, out):
         x_tiles = [keep.tile([P, 2 * (hi - lo)], U8, align_bytes=64, name=f"x{lo}") for lo, hi in LOADS]
         planes = [keep.tile([P, hi - lo], U8, align_bytes=64, name=f"plane{lo}") for lo, hi in LOADS]
         window = keep.tile([P, U], F32)
-        warm_in = keep.tile([P, 1], F32)
-        warm_out = keep.tile([P, 1], F32)
 
         def load_scales(queue, i, q):
             lo, hi = LOADS[i]
             queue.dma_start(
-                out=planes[i][32 * q : 32 * q + 4, :].bitcast(I32),
-                in_=x_scales[0, 4 * q : 4 * q + 4, lo:hi].bitcast(I32),
+                out=planes[i][q:P:32, :].bitcast(I32),
+                in_=x_scales[0, q:16:4, lo:hi].bitcast(I32),
             )
 
         def load_words(queue, i):
@@ -60,9 +58,6 @@ def tile_picked_wkvput_tanh_l_kernel(tc, x_words, x_scales, mem, w1, slot, out):
         load_words(nc.sync, 1)
         for q in range(4):
             load_scales(nc.sync, 1, q)
-
-        nc.vector.memset(warm_in[:], 0.0)
-        nc.scalar.activation(warm_out[:], warm_in[:], TANH)
 
         w_grouped = keep.tile([P, M, PACK], BF16, align_bytes=64)
         w_codes = keep.tile([P, M], U32, align_bytes=64)

@@ -17,9 +17,10 @@ TANH = mybir.ActivationFunctionType.Tanh
 
 P = 128
 PACK = 4
-LOADS = ((0, 384), (384, 1024))
-PASSES = ((0, 256), (256, 384), (384, 640), (640, 896), (896, 1024))
-SCATTERS = (384, 1024)
+WORD_LOADS = ((0, 256), (256, 512), (512, 768), (768, 1024))
+SCALE_LOADS = ((0, 512), (512, 1024))
+PASSES = ((0, 256), (256, 512), (512, 768), (768, 1024))
+SCATTERS = (256, 1024)
 HALVES = ((0, 64), (64, 128))
 STORES = ((0, 2048),)
 
@@ -32,19 +33,19 @@ def tile_picked_wkvput_tanh_l_kernel(tc, x_words, x_scales, mem, w1, slot, out):
 
         offsets = keep.tile([P, T // 16], U16)
         w_raw = keep.tile([P, PACK, M], F32)
-        x_tiles = [keep.tile([P, 2 * (hi - lo)], U8, align_bytes=64, name=f"x{lo}") for lo, hi in LOADS]
-        planes = [keep.tile([P, hi - lo], U8, align_bytes=64, name=f"plane{lo}") for lo, hi in LOADS]
+        x_tiles = [keep.tile([P, 2 * (hi - lo)], U8, align_bytes=64, name=f"x{lo}") for lo, hi in WORD_LOADS]
+        planes = [keep.tile([P, hi - lo], U8, align_bytes=64, name=f"plane{lo}") for lo, hi in SCALE_LOADS]
         window = keep.tile([P, U], F32)
 
         def load_scales(queue, i, q):
-            lo, hi = LOADS[i]
+            lo, hi = SCALE_LOADS[i]
             queue.dma_start(
                 out=planes[i][q:P:32, :].bitcast(I32),
                 in_=x_scales[0, q:16:4, lo:hi].bitcast(I32),
             )
 
         def load_words(queue, i):
-            lo, hi = LOADS[i]
+            lo, hi = WORD_LOADS[i]
             queue.dma_start(out=x_tiles[i][:], in_=x_words[0, :, 2 * lo : 2 * hi])
 
         nc.sync.dma_start(out=w_raw[:], in_=w1.rearrange("(p j) m -> p j m", j=PACK))
@@ -53,11 +54,13 @@ def tile_picked_wkvput_tanh_l_kernel(tc, x_words, x_scales, mem, w1, slot, out):
         load_words(nc.sync, 0)
         load_scales(nc.sync, 0, 2)
         load_scales(nc.sync, 0, 3)
-        nc.sync.dma_start(out=window[:], in_=mem)
         nc.sync.dma_start(offsets[:], slot)
+        nc.sync.dma_start(out=window[:], in_=mem)
         load_words(nc.sync, 1)
         for q in range(4):
             load_scales(nc.sync, 1, q)
+        load_words(nc.sync, 2)
+        load_words(nc.sync, 3)
 
         w_grouped = keep.tile([P, M, PACK], BF16, align_bytes=64)
         w_codes = keep.tile([P, M], U32, align_bytes=64)
@@ -77,14 +80,15 @@ def tile_picked_wkvput_tanh_l_kernel(tc, x_words, x_scales, mem, w1, slot, out):
         y = keep.tile([P, T], F32)
         done = 0
         for lo, hi in PASSES:
-            tile, plane, base = [(t, s, a) for t, s, (a, b) in zip(x_tiles, planes, LOADS) if a <= lo and hi <= b][0]
+            tile, base = [(t, a) for t, (a, b) in zip(x_tiles, WORD_LOADS) if a <= lo and hi <= b][0]
+            plane, plane_base = [(s, a) for s, (a, b) in zip(planes, SCALE_LOADS) if a <= lo and hi <= b][0]
             acc = psum.tile([P, hi - lo], F32, name=f"acc{lo}")
             nc.tensor.matmul_mx(
                 out=acc[:],
                 lhsT=w_codes[:].bitcast(FP8X4),
                 lhsT_scale=w_plane[:],
                 rhs=tile[:, 2 * (lo - base) : 2 * (hi - base)].bitcast(FP4X4),
-                rhs_scale=plane[:, lo - base : hi - base],
+                rhs_scale=plane[:, lo - plane_base : hi - plane_base],
                 start=True,
                 stop=True,
             )

@@ -19,7 +19,7 @@ P = 128
 PACK = 4
 WORD_LOADS = ((0, 256), (256, 512), (512, 768), (768, 1024))
 SCALE_LOADS = ((0, 512), (512, 1024))
-PASSES = ((0, 256), (256, 512), (512, 768), (768, 1024))
+PASSES = ((0, 128), (128, 256), (256, 512), (512, 768), (768, 896), (896, 1024))
 SCATTERS = (256, 1024)
 HALVES = ((0, 64), (64, 128))
 STORES = ((0, 2048),)
@@ -31,11 +31,11 @@ def tile_picked_wkvput_tanh_l_kernel(tc, x_words, x_scales, mem, w1, slot, out):
         keep = ctx.enter_context(tc.tile_pool(name="keep", bufs=1))
         psum = ctx.enter_context(tc.psum_pool(name="psum", bufs=1))
 
-        offsets = keep.tile([P, T // 16], U16)
-        w_raw = keep.tile([P, PACK, M], F32)
-        x_tiles = [keep.tile([P, 2 * (hi - lo)], U8, align_bytes=64, name=f"x{lo}") for lo, hi in WORD_LOADS]
-        planes = [keep.tile([P, hi - lo], U8, align_bytes=64, name=f"plane{lo}") for lo, hi in SCALE_LOADS]
-        window = keep.tile([P, U], F32)
+        offsets = keep.tile([P, T // 16], U16, align_bytes=256)
+        w_raw = keep.tile([P, PACK, M], F32, align_bytes=256)
+        x_tiles = [keep.tile([P, 2 * (hi - lo)], U8, align_bytes=256, name=f"x{lo}") for lo, hi in WORD_LOADS]
+        planes = [keep.tile([P, hi - lo], U8, align_bytes=256, name=f"plane{lo}") for lo, hi in SCALE_LOADS]
+        window = keep.tile([P, U], F32, align_bytes=256)
 
         def load_scales(queue, i, q):
             lo, hi = SCALE_LOADS[i]

@@ -18,7 +18,7 @@ TANH = mybir.ActivationFunctionType.Tanh
 P = 128
 PACK = 4
 WORD_LOADS = ((0, 256), (256, 512), (512, 768), (768, 1024))
-SCALE_LOADS = ((0, 512), (512, 1024))
+SCALE_LOADS = ((0, 768), (768, 1024))
 PASSES = ((0, 128), (128, 256), (256, 512), (512, 768), (768, 896), (896, 1024))
 SCATTERS = (256, 1024)
 HALVES = ((0, 64), (64, 128))
@@ -57,9 +57,9 @@ def tile_picked_wkvput_tanh_l_kernel(tc, x_words, x_scales, mem, w1, slot, out):
         nc.sync.dma_start(offsets[:], slot)
         nc.sync.dma_start(out=window[:], in_=mem)
         load_words(nc.sync, 1)
+        load_words(nc.sync, 2)
         for q in range(4):
             load_scales(nc.sync, 1, q)
-        load_words(nc.sync, 2)
         load_words(nc.sync, 3)
 
         w_grouped = keep.tile([P, M, PACK], BF16, align_bytes=64)

@@ -1,6 +1,7 @@
 from contextlib import ExitStack
 
 import concourse.mybir as mybir
+from concourse.masks import make_identity
 
 K, T, M, U = 512, 1024, 128, 2048
 FLOPS = 2 * K * M * T
@@ -13,16 +14,22 @@ U16 = mybir.dt.uint16
 U8 = mybir.dt.uint8
 FP8X4 = mybir.dt.float8_e4m3fn_x4
 FP4X4 = mybir.dt.float4_e2m1fn_x4
-TANH = mybir.ActivationFunctionType.Tanh
+ACT = mybir.ActivationFunctionType
+ALU = mybir.AluOpType
 
 P = 128
 PACK = 4
-WORD_LOADS = ((0, 256), (256, 512), (512, 768), (768, 1024))
-SCALE_LOADS = ((0, 768), (768, 1024))
-PASSES = ((0, 128), (128, 256), (256, 512), (512, 768), (768, 896), (896, 1024))
-SCATTERS = (256, 1024)
+BANK = 512
+HALF = BANK // 2
+WORD_LOADS = ((0, 256), (256, 1024))
+PASSES = ((0, 128), (128, 256), (256, 512), (512, 640), (640, 896), (896, 1024))
+VECTOR_SCATTERS = ((0, 256), (256, 640))
+SCALAR_SCATTER = (640, 1024)
 HALVES = ((0, 64), (64, 128))
-STORES = ((0, 2048),)
+TURNED = ((0, 256), (256, 512))
+DIRECT = ((512, 768), (768, 1280), (1280, 1536), (1536, 1792), (1792, 2048))
+LIFT = 2.0**60
+FILLER = 2.0**-100
 
 
 def tile_picked_wkvput_tanh_l_kernel(tc, x_words, x_scales, mem, w1, slot, out):
@@ -34,33 +41,33 @@ def tile_picked_wkvput_tanh_l_kernel(tc, x_words, x_scales, mem, w1, slot, out):
         offsets = keep.tile([P, T // 16], U16, align_bytes=256)
         w_raw = keep.tile([P, PACK, M], F32, align_bytes=256)
         x_tiles = [keep.tile([P, 2 * (hi - lo)], U8, align_bytes=256, name=f"x{lo}") for lo, hi in WORD_LOADS]
-        planes = [keep.tile([P, hi - lo], U8, align_bytes=256, name=f"plane{lo}") for lo, hi in SCALE_LOADS]
+        plane = keep.tile([P, T], U8, align_bytes=256)
         window = keep.tile([P, U], F32, align_bytes=256)
+        side = keep.tile([P, U], F32, align_bytes=256)
+        lift = keep.tile([P, max(hi - lo for lo, hi in VECTOR_SCATTERS)], F32, align_bytes=256)
+        ident = keep.tile([P, P], F32, align_bytes=256)
+        banks = [psum.tile([P, BANK], F32, name=f"bank{b}") for b in range(8)]
 
-        def load_scales(queue, i, q):
-            lo, hi = SCALE_LOADS[i]
-            queue.dma_start(
-                out=planes[i][q:P:32, :].bitcast(I32),
-                in_=x_scales[0, q:16:4, lo:hi].bitcast(I32),
-            )
+        def load_scales(queue, q):
+            queue.dma_start(out=plane[q:P:32, :].bitcast(I32), in_=x_scales[0, q:16:4, :].bitcast(I32))
 
-        def load_words(queue, i):
+        def load_words(i):
             lo, hi = WORD_LOADS[i]
-            queue.dma_start(out=x_tiles[i][:], in_=x_words[0, :, 2 * lo : 2 * hi])
+            nc.sync.dma_start(out=x_tiles[i][:], in_=x_words[0, :, 2 * lo : 2 * hi])
 
         nc.sync.dma_start(out=w_raw[:], in_=w1.rearrange("(p j) m -> p j m", j=PACK))
-        load_scales(nc.scalar, 0, 0)
-        load_scales(nc.scalar, 0, 1)
-        load_words(nc.sync, 0)
-        load_scales(nc.sync, 0, 2)
-        load_scales(nc.sync, 0, 3)
+        load_scales(nc.scalar, 0)
+        load_scales(nc.scalar, 1)
+        load_words(0)
+        load_scales(nc.sync, 2)
+        load_scales(nc.sync, 3)
+        load_words(1)
         nc.sync.dma_start(offsets[:], slot)
         nc.sync.dma_start(out=window[:], in_=mem)
-        load_words(nc.sync, 1)
-        load_words(nc.sync, 2)
-        for q in range(4):
-            load_scales(nc.sync, 1, q)
-        load_words(nc.sync, 3)
+
+        nc.vector.memset(side[:], FILLER)
+        nc.vector.memset(lift[:], LIFT)
+        make_identity(nc, ident[:])
 
         w_grouped = keep.tile([P, M, PACK], BF16, align_bytes=64)
         w_codes = keep.tile([P, M], U32, align_bytes=64)
@@ -77,26 +84,97 @@ def tile_picked_wkvput_tanh_l_kernel(tc, x_words, x_scales, mem, w1, slot, out):
                 in_=w_grouped[:, lo:hi, :].rearrange("p m j -> p (m j)"),
             )
 
-        y = keep.tile([P, T], F32)
-        done = 0
-        for lo, hi in PASSES:
+        y = keep.tile([P, T], F32, align_bytes=256)
+        for i, (lo, hi) in enumerate(PASSES):
             tile, base = [(t, a) for t, (a, b) in zip(x_tiles, WORD_LOADS) if a <= lo and hi <= b][0]
-            plane, plane_base = [(s, a) for s, (a, b) in zip(planes, SCALE_LOADS) if a <= lo and hi <= b][0]
-            acc = psum.tile([P, hi - lo], F32, name=f"acc{lo}")
+            acc = banks[i][:, : hi - lo]
             nc.tensor.matmul_mx(
-                out=acc[:],
+                out=acc,
                 lhsT=w_codes[:].bitcast(FP8X4),
                 lhsT_scale=w_plane[:],
                 rhs=tile[:, 2 * (lo - base) : 2 * (hi - base)].bitcast(FP4X4),
-                rhs_scale=plane[:, lo - plane_base : hi - plane_base],
+                rhs_scale=plane[:, lo:hi],
                 start=True,
                 stop=True,
             )
-            nc.scalar.activation(y[:, lo:hi], acc[:], TANH)
-            if hi in SCATTERS:
-                nc.vector.tensor_copy(window[:].indirect(offsets[:, done // 16 : hi // 16]), y[:, done:hi])
-                done = hi
+            nc.scalar.activation(y[:, lo:hi], acc, ACT.Tanh)
+            for a, b in VECTOR_SCATTERS:
+                if b == hi:
+                    nc.vector.tensor_tensor(
+                        side[:].indirect(offsets[:, a // 16 : b // 16]), y[:, a:b], lift[:, : b - a], ALU.mult
+                    )
+        a, b = SCALAR_SCATTER
+        nc.scalar.activation(window[:].indirect(offsets[:, a // 16 : b // 16]), y[:, a:b], ACT.Copy)
 
-        for s, (lo, hi) in enumerate(STORES):
-            queue = nc.sync if s % 2 == 0 else nc.scalar
-            queue.dma_start(out=out[:, lo:hi], in_=window[:, lo:hi])
+        def clear(lo, hi):
+            nc.vector.scalar_tensor_tensor(
+                window[:, lo:hi], side[:, lo:hi], FILLER, window[:, lo:hi], ALU.is_equal, ALU.mult
+            )
+
+        def add(lo, hi):
+            nc.vector.scalar_tensor_tensor(
+                window[:, lo:hi], side[:, lo:hi], 1.0 / LIFT, window[:, lo:hi], ALU.mult, ALU.add
+            )
+            nc.sync.dma_start(out=out[:, lo:hi], in_=window[:, lo:hi])
+
+        def blocks(g):
+            lo, hi = TURNED[g]
+            return [(c - lo, c) for c in range(lo, hi, P)]
+
+        new_t = [keep.tile([P, hi - lo], F32, align_bytes=256, name=f"new{lo}") for lo, hi in TURNED]
+        old_t = [keep.tile([P, hi - lo], F32, align_bytes=256, name=f"old{lo}") for lo, hi in TURNED]
+        kept = [keep.tile([P, (hi - lo) // P], F32, align_bytes=32, name=f"kept{lo}") for lo, hi in TURNED]
+
+        gap = [keep.tile([P, (hi - lo) // P], F32, align_bytes=32, name=f"gap{lo}") for lo, hi in TURNED]
+        written = [keep.tile([P, (hi - lo) // P], F32, align_bytes=32, name=f"written{lo}") for lo, hi in TURNED]
+
+        def turn_old(g):
+            for j, c in blocks(g):
+                nc.tensor.transpose(banks[g][:, j : j + P], window[:, c : c + P], ident[:])
+
+        def turn_new(g):
+            for j, c in blocks(g):
+                nc.tensor.transpose(banks[g][:, HALF + j : HALF + j + P], side[:, c : c + P], ident[:])
+
+        def choose(g):
+            lo, hi = TURNED[g]
+            turned_new = banks[g][:, HALF : HALF + hi - lo]
+            nc.scalar.activation(gap[g][:], turned_new[:, ::P], ACT.Sign, bias=-FILLER)
+            nc.scalar.activation(new_t[g][:], turned_new, ACT.Copy, scale=1.0 / LIFT)
+            nc.scalar.activation(written[g][:], gap[g][:], ACT.Square)
+            nc.scalar.activation(kept[g][:], written[g][:], ACT.Identity, bias=1.0, scale=-1.0)
+            for j, c in blocks(g):
+                nc.scalar.activation(
+                    old_t[g][:, j : j + P], banks[g][:, j : j + P], ACT.Copy, scale=kept[g][:, j // P : j // P + 1]
+                )
+
+        def turn_back(g):
+            lo, hi = TURNED[g]
+            bank = banks[4 + g]
+            for j, c in blocks(g):
+                nc.tensor.matmul(
+                    bank[:, j : j + P], lhsT=new_t[g][:, j : j + P], rhs=ident[:], is_transpose=True, start=(j == 0), stop=False
+                )
+            for j, c in blocks(g):
+                nc.tensor.matmul(
+                    bank[:, j : j + P], lhsT=old_t[g][:, j : j + P], rhs=ident[:], is_transpose=True, start=False, stop=(c + P == hi)
+                )
+
+        def leave(g):
+            lo, hi = TURNED[g]
+            nc.scalar.copy(window[:, lo:hi], banks[4 + g][:, : hi - lo])
+            nc.sync.dma_start(out=out[:, lo:hi], in_=window[:, lo:hi])
+
+        for g in range(len(TURNED)):
+            turn_old(g)
+        for g in range(len(TURNED)):
+            turn_new(g)
+            choose(g)
+        clear(*DIRECT[0])
+        for i in range(len(DIRECT)):
+            if i + 1 < len(DIRECT):
+                clear(*DIRECT[i + 1])
+            add(*DIRECT[i])
+        for g in range(len(TURNED)):
+            turn_back(g)
+            leave(g)

@@ -20,16 +20,16 @@ ALU = mybir.AluOpType
 P = 128
 PACK = 4
 BANK = 512
-HALF = BANK // 2
 WORD_LOADS = ((0, 256), (256, 1024))
 PASSES = ((0, 128), (128, 256), (256, 512), (512, 640), (640, 896), (896, 1024))
-VECTOR_SCATTERS = ((0, 256), (256, 640))
+VECTOR_SCATTERS = ((0, 128), (128, 640))
 SCALAR_SCATTER = (640, 1024)
 HALVES = ((0, 64), (64, 128))
-TURNED = ((0, 256), (256, 512))
-DIRECT = ((512, 768), (768, 1280), (1280, 1536), (1536, 1792), (1792, 2048))
-LIFT = 2.0**60
-FILLER = 2.0**-100
+DIRECT = ((0, 256), (256, 768), (768, 1024), (1024, 1280), (1792, 2048))
+TURNED = ((1280, 1536), (1536, 1792))
+STORES = ((0, 256), (256, 768), (768, 1024), (1024, 1280), (1280, 1536), (1536, 1792), (1792, 2048))
+SHIFT = 2.0**-100
+FILLER = 2.0**-126
 
 
 def tile_picked_wkvput_tanh_l_kernel(tc, x_words, x_scales, mem, w1, slot, out):
@@ -44,7 +44,7 @@ def tile_picked_wkvput_tanh_l_kernel(tc, x_words, x_scales, mem, w1, slot, out):
         plane = keep.tile([P, T], U8, align_bytes=256)
         window = keep.tile([P, U], F32, align_bytes=256)
         side = keep.tile([P, U], F32, align_bytes=256)
-        lift = keep.tile([P, max(hi - lo for lo, hi in VECTOR_SCATTERS)], F32, align_bytes=256)
+        const = keep.tile([P, max(hi - lo for lo, hi in VECTOR_SCATTERS)], F32, align_bytes=256)
         ident = keep.tile([P, P], F32, align_bytes=256)
         banks = [psum.tile([P, BANK], F32, name=f"bank{b}") for b in range(8)]
 
@@ -65,8 +65,9 @@ def tile_picked_wkvput_tanh_l_kernel(tc, x_words, x_scales, mem, w1, slot, out):
         nc.sync.dma_start(offsets[:], slot)
         nc.sync.dma_start(out=window[:], in_=mem)
 
-        nc.vector.memset(side[:], FILLER)
-        nc.vector.memset(lift[:], LIFT)
+        nc.vector.memset(side[:, : U // 2], FILLER)
+        nc.vector.memset(const[:], SHIFT)
+        nc.scalar.activation(side[:, U // 2 :], side[:, : U // 2], ACT.Copy)
         make_identity(nc, ident[:])
 
         w_grouped = keep.tile([P, M, PACK], BF16, align_bytes=64)
@@ -101,10 +102,18 @@ def tile_picked_wkvput_tanh_l_kernel(tc, x_words, x_scales, mem, w1, slot, out):
             for a, b in VECTOR_SCATTERS:
                 if b == hi:
                     nc.vector.tensor_tensor(
-                        side[:].indirect(offsets[:, a // 16 : b // 16]), y[:, a:b], lift[:, : b - a], ALU.mult
+                        side[:].indirect(offsets[:, a // 16 : b // 16]), y[:, a:b], const[:, : b - a], ALU.add
                     )
         a, b = SCALAR_SCATTER
         nc.scalar.activation(window[:].indirect(offsets[:, a // 16 : b // 16]), y[:, a:b], ACT.Copy)
+
+        stored = []
+
+        def finished(lo, hi):
+            stored.append((lo, hi))
+            for a, b in STORES:
+                if a <= lo and hi <= b and sum(d - c for c, d in stored if a <= c and d <= b) == b - a:
+                    nc.sync.dma_start(out=out[:, a:b], in_=window[:, a:b])
 
         def clear(lo, hi):
             nc.vector.scalar_tensor_tensor(
@@ -112,69 +121,80 @@ def tile_picked_wkvput_tanh_l_kernel(tc, x_words, x_scales, mem, w1, slot, out):
             )
 
         def add(lo, hi):
-            nc.vector.scalar_tensor_tensor(
-                window[:, lo:hi], side[:, lo:hi], 1.0 / LIFT, window[:, lo:hi], ALU.mult, ALU.add
-            )
-            nc.sync.dma_start(out=out[:, lo:hi], in_=window[:, lo:hi])
+            nc.vector.tensor_tensor(window[:, lo:hi], side[:, lo:hi], window[:, lo:hi], ALU.add)
+            finished(lo, hi)
 
-        def blocks(g):
-            lo, hi = TURNED[g]
-            return [(c - lo, c) for c in range(lo, hi, P)]
-
+        groups = range(len(TURNED))
         new_t = [keep.tile([P, hi - lo], F32, align_bytes=256, name=f"new{lo}") for lo, hi in TURNED]
         old_t = [keep.tile([P, hi - lo], F32, align_bytes=256, name=f"old{lo}") for lo, hi in TURNED]
-        kept = [keep.tile([P, (hi - lo) // P], F32, align_bytes=32, name=f"kept{lo}") for lo, hi in TURNED]
-
-        gap = [keep.tile([P, (hi - lo) // P], F32, align_bytes=32, name=f"gap{lo}") for lo, hi in TURNED]
+        differs = [keep.tile([P, (hi - lo) // P], F32, align_bytes=32, name=f"differs{lo}") for lo, hi in TURNED]
         written = [keep.tile([P, (hi - lo) // P], F32, align_bytes=32, name=f"written{lo}") for lo, hi in TURNED]
+        kept = [keep.tile([P, (hi - lo) // P], F32, align_bytes=32, name=f"kept{lo}") for lo, hi in TURNED]
+        HALF = BANK // 2
 
-        def turn_old(g):
-            for j, c in blocks(g):
-                nc.tensor.transpose(banks[g][:, j : j + P], window[:, c : c + P], ident[:])
-
-        def turn_new(g):
-            for j, c in blocks(g):
-                nc.tensor.transpose(banks[g][:, HALF + j : HALF + j + P], side[:, c : c + P], ident[:])
-
-        def choose(g):
+        def turn(g, tile, at):
             lo, hi = TURNED[g]
-            turned_new = banks[g][:, HALF : HALF + hi - lo]
-            nc.scalar.activation(gap[g][:], turned_new[:, ::P], ACT.Sign, bias=-FILLER)
-            nc.scalar.activation(new_t[g][:], turned_new, ACT.Copy, scale=1.0 / LIFT)
-            nc.scalar.activation(written[g][:], gap[g][:], ACT.Square)
+            for c in range(lo, hi, P):
+                nc.tensor.transpose(banks[g][:, at + c - lo : at + c - lo + P], tile[:, c : c + P], ident[:])
+
+        def sign(g):
+            lo, hi = TURNED[g]
+            nc.scalar.activation(differs[g][:], banks[g][:, HALF : HALF + hi - lo : P], ACT.Sign, bias=-FILLER)
+
+        def take_new(g):
+            lo, hi = TURNED[g]
+            nc.scalar.activation(new_t[g][:], banks[g][:, HALF : HALF + hi - lo], ACT.Copy)
+
+        def square(g):
+            nc.scalar.activation(written[g][:], differs[g][:], ACT.Square)
+
+        def flip(g):
             nc.scalar.activation(kept[g][:], written[g][:], ACT.Identity, bias=1.0, scale=-1.0)
-            for j, c in blocks(g):
+
+        def take_old(g):
+            lo, hi = TURNED[g]
+            for j in range(0, hi - lo, P):
                 nc.scalar.activation(
                     old_t[g][:, j : j + P], banks[g][:, j : j + P], ACT.Copy, scale=kept[g][:, j // P : j // P + 1]
                 )
 
-        def turn_back(g):
+        def turn_back(g, tile, first):
             lo, hi = TURNED[g]
-            bank = banks[4 + g]
-            for j, c in blocks(g):
+            for j in range(0, hi - lo, P):
                 nc.tensor.matmul(
-                    bank[:, j : j + P], lhsT=new_t[g][:, j : j + P], rhs=ident[:], is_transpose=True, start=(j == 0), stop=False
-                )
-            for j, c in blocks(g):
-                nc.tensor.matmul(
-                    bank[:, j : j + P], lhsT=old_t[g][:, j : j + P], rhs=ident[:], is_transpose=True, start=False, stop=(c + P == hi)
+                    banks[4 + g][:, j : j + P],
+                    lhsT=tile[:, j : j + P],
+                    rhs=ident[:],
+                    is_transpose=True,
+                    start=(first and j == 0),
+                    stop=(not first and lo + j + P == hi),
                 )
 
         def leave(g):
             lo, hi = TURNED[g]
             nc.scalar.copy(window[:, lo:hi], banks[4 + g][:, : hi - lo])
-            nc.sync.dma_start(out=out[:, lo:hi], in_=window[:, lo:hi])
+            finished(lo, hi)
 
-        for g in range(len(TURNED)):
-            turn_old(g)
-        for g in range(len(TURNED)):
-            turn_new(g)
-            choose(g)
+        for g in groups:
+            turn(g, window, 0)
+        for g in groups:
+            turn(g, side, HALF)
+        sign(0)
+        take_new(0)
+        square(0)
+        sign(1)
+        flip(0)
+        square(1)
+        take_old(0)
+        flip(1)
+        take_new(1)
+        take_old(1)
+        for g in groups:
+            turn_back(g, new_t[g], True)
+            turn_back(g, old_t[g], False)
+            leave(g)
         clear(*DIRECT[0])
         for i in range(len(DIRECT)):
             if i + 1 < len(DIRECT):
                 clear(*DIRECT[i + 1])
             add(*DIRECT[i])
-        for g in range(len(TURNED)):
-            turn_back(g)
-            leave(g)

@@ -27,7 +27,6 @@ SCALAR_SCATTER = (640, 1024)
 HALVES = ((0, 64), (64, 128))
 DIRECT = ((0, 256), (256, 768), (768, 1024), (1024, 1280), (1792, 2048))
 TURNED = ((1280, 1536), (1536, 1792))
-STORES = ((0, 256), (256, 768), (768, 1024), (1024, 1280), (1280, 1536), (1536, 1792), (1792, 2048))
 SHIFT = 2.0**-100
 FILLER = 2.0**-126
 
@@ -107,14 +106,6 @@ def tile_picked_wkvput_tanh_l_kernel(tc, x_words, x_scales, mem, w1, slot, out):
         a, b = SCALAR_SCATTER
         nc.scalar.activation(window[:].indirect(offsets[:, a // 16 : b // 16]), y[:, a:b], ACT.Copy)
 
-        stored = []
-
-        def finished(lo, hi):
-            stored.append((lo, hi))
-            for a, b in STORES:
-                if a <= lo and hi <= b and sum(d - c for c, d in stored if a <= c and d <= b) == b - a:
-                    nc.sync.dma_start(out=out[:, a:b], in_=window[:, a:b])
-
         def clear(lo, hi):
             nc.vector.scalar_tensor_tensor(
                 window[:, lo:hi], side[:, lo:hi], FILLER, window[:, lo:hi], ALU.is_equal, ALU.mult
@@ -122,7 +113,7 @@ def tile_picked_wkvput_tanh_l_kernel(tc, x_words, x_scales, mem, w1, slot, out):
 
         def add(lo, hi):
             nc.vector.tensor_tensor(window[:, lo:hi], side[:, lo:hi], window[:, lo:hi], ALU.add)
-            finished(lo, hi)
+            nc.sync.dma_start(out=out[:, lo:hi], in_=window[:, lo:hi])
 
         groups = range(len(TURNED))
         new_t = [keep.tile([P, hi - lo], F32, align_bytes=256, name=f"new{lo}") for lo, hi in TURNED]
@@ -173,7 +164,7 @@ def tile_picked_wkvput_tanh_l_kernel(tc, x_words, x_scales, mem, w1, slot, out):
         def leave(g):
             lo, hi = TURNED[g]
             nc.scalar.copy(window[:, lo:hi], banks[4 + g][:, : hi - lo])
-            finished(lo, hi)
+            nc.scalar.dma_start(out=out[:, lo:hi], in_=window[:, lo:hi])
 
         for g in groups:
             turn(g, window, 0)
@@ -189,12 +180,12 @@ def tile_picked_wkvput_tanh_l_kernel(tc, x_words, x_scales, mem, w1, slot, out):
         flip(1)
         take_new(1)
         take_old(1)
-        for g in groups:
-            turn_back(g, new_t[g], True)
-            turn_back(g, old_t[g], False)
-            leave(g)
         clear(*DIRECT[0])
         for i in range(len(DIRECT)):
             if i + 1 < len(DIRECT):
                 clear(*DIRECT[i + 1])
             add(*DIRECT[i])
+        for g in groups:
+            turn_back(g, new_t[g], True)
+            turn_back(g, old_t[g], False)
+            leave(g)

@@ -21,12 +21,13 @@ P = 128
 PACK = 4
 BANK = 512
 WORD_LOADS = ((0, 256), (256, 1024))
-PASSES = ((0, 128), (128, 256), (256, 512), (512, 640), (640, 896), (896, 1024))
-VECTOR_SCATTERS = ((0, 128), (128, 640))
-SCALAR_SCATTER = (640, 1024)
+PASSES = ((0, 128), (128, 256), (256, 512), (640, 896), (512, 640), (896, 1024))
+FIRST = (0, 128)
+OVER_MEM = (128, 640)
+BY_SCALAR = (640, 1024)
 HALVES = ((0, 64), (64, 128))
-DIRECT = ((0, 256), (256, 768), (768, 1024), (1024, 1280), (1792, 2048))
-TURNED = ((1280, 1536), (1536, 1792))
+DIRECT = ((0, 128), (128, 384), (384, 640), (640, 896), (896, 1152), (1152, 1408))
+TURNED = ((1408, 1664), (1664, 2048))
 SHIFT = 2.0**-100
 FILLER = 2.0**-126
 
@@ -43,29 +44,29 @@ def tile_picked_wkvput_tanh_l_kernel(tc, x_words, x_scales, mem, w1, slot, out):
         plane = keep.tile([P, T], U8, align_bytes=256)
         window = keep.tile([P, U], F32, align_bytes=256)
         side = keep.tile([P, U], F32, align_bytes=256)
-        const = keep.tile([P, max(hi - lo for lo, hi in VECTOR_SCATTERS)], F32, align_bytes=256)
+        shift = keep.tile([P, FIRST[1] - FIRST[0]], F32, align_bytes=256)
         ident = keep.tile([P, P], F32, align_bytes=256)
         banks = [psum.tile([P, BANK], F32, name=f"bank{b}") for b in range(8)]
 
         def load_scales(queue, q):
             queue.dma_start(out=plane[q:P:32, :].bitcast(I32), in_=x_scales[0, q:16:4, :].bitcast(I32))
 
-        def load_words(i):
+        def load_words(queue, i):
             lo, hi = WORD_LOADS[i]
-            nc.sync.dma_start(out=x_tiles[i][:], in_=x_words[0, :, 2 * lo : 2 * hi])
+            queue.dma_start(out=x_tiles[i][:].bitcast(I32), in_=x_words[0, :, 2 * lo : 2 * hi].bitcast(I32))
 
         nc.sync.dma_start(out=w_raw[:], in_=w1.rearrange("(p j) m -> p j m", j=PACK))
         load_scales(nc.scalar, 0)
         load_scales(nc.scalar, 1)
-        load_words(0)
+        load_words(nc.gpsimd, 1)
+        load_words(nc.sync, 0)
         load_scales(nc.sync, 2)
         load_scales(nc.sync, 3)
-        load_words(1)
         nc.sync.dma_start(offsets[:], slot)
         nc.sync.dma_start(out=window[:], in_=mem)
 
         nc.vector.memset(side[:, : U // 2], FILLER)
-        nc.vector.memset(const[:], SHIFT)
+        nc.vector.memset(shift[:], SHIFT)
         nc.scalar.activation(side[:, U // 2 :], side[:, : U // 2], ACT.Copy)
         make_identity(nc, ident[:])
 
@@ -97,14 +98,17 @@ def tile_picked_wkvput_tanh_l_kernel(tc, x_words, x_scales, mem, w1, slot, out):
                 start=True,
                 stop=True,
             )
-            nc.scalar.activation(y[:, lo:hi], acc, ACT.Tanh)
-            for a, b in VECTOR_SCATTERS:
-                if b == hi:
-                    nc.vector.tensor_tensor(
-                        side[:].indirect(offsets[:, a // 16 : b // 16]), y[:, a:b], const[:, : b - a], ALU.add
-                    )
-        a, b = SCALAR_SCATTER
-        nc.scalar.activation(window[:].indirect(offsets[:, a // 16 : b // 16]), y[:, a:b], ACT.Copy)
+            if lo >= BY_SCALAR[0]:
+                nc.scalar.activation(y[:, lo:hi], acc, ACT.Tanh, bias=SHIFT)
+            else:
+                nc.scalar.activation(y[:, lo:hi], acc, ACT.Tanh)
+
+        def picks(piece):
+            return offsets[:, piece[0] // 16 : piece[1] // 16]
+
+        nc.vector.tensor_tensor(side[:].indirect(picks(FIRST)), y[:, FIRST[0] : FIRST[1]], shift[:], ALU.add)
+        nc.vector.tensor_copy(window[:].indirect(picks(OVER_MEM)), y[:, OVER_MEM[0] : OVER_MEM[1]])
+        nc.scalar.activation(side[:].indirect(picks(BY_SCALAR)), y[:, BY_SCALAR[0] : BY_SCALAR[1]], ACT.Copy)
 
         def clear(lo, hi):
             nc.vector.scalar_tensor_tensor(
@@ -118,42 +122,38 @@ def tile_picked_wkvput_tanh_l_kernel(tc, x_words, x_scales, mem, w1, slot, out):
         groups = range(len(TURNED))
         new_t = [keep.tile([P, hi - lo], F32, align_bytes=256, name=f"new{lo}") for lo, hi in TURNED]
         old_t = [keep.tile([P, hi - lo], F32, align_bytes=256, name=f"old{lo}") for lo, hi in TURNED]
-        differs = [keep.tile([P, (hi - lo) // P], F32, align_bytes=32, name=f"differs{lo}") for lo, hi in TURNED]
-        written = [keep.tile([P, (hi - lo) // P], F32, align_bytes=32, name=f"written{lo}") for lo, hi in TURNED]
+        away = [keep.tile([P, (hi - lo) // P], F32, align_bytes=32, name=f"away{lo}") for lo, hi in TURNED]
         kept = [keep.tile([P, (hi - lo) // P], F32, align_bytes=32, name=f"kept{lo}") for lo, hi in TURNED]
-        HALF = BANK // 2
+        side_banks, mem_banks, sum_banks = banks[6:8], banks[0:2], banks[2:4]
 
-        def turn(g, tile, at):
+        def turn(g, tile, bank):
             lo, hi = TURNED[g]
             for c in range(lo, hi, P):
-                nc.tensor.transpose(banks[g][:, at + c - lo : at + c - lo + P], tile[:, c : c + P], ident[:])
+                nc.tensor.transpose(bank[:, c - lo : c - lo + P], tile[:, c : c + P], ident[:])
 
-        def sign(g):
+        def measure(g):
             lo, hi = TURNED[g]
-            nc.scalar.activation(differs[g][:], banks[g][:, HALF : HALF + hi - lo : P], ACT.Sign, bias=-FILLER)
+            nc.scalar.activation(away[g][:], side_banks[g][:, : hi - lo : P], ACT.Abs, bias=-1.0, scale=1.0 / FILLER)
 
         def take_new(g):
             lo, hi = TURNED[g]
-            nc.scalar.activation(new_t[g][:], banks[g][:, HALF : HALF + hi - lo], ACT.Copy)
+            nc.scalar.activation(new_t[g][:], side_banks[g][:, : hi - lo], ACT.Copy)
 
-        def square(g):
-            nc.scalar.activation(written[g][:], differs[g][:], ACT.Square)
-
-        def flip(g):
-            nc.scalar.activation(kept[g][:], written[g][:], ACT.Identity, bias=1.0, scale=-1.0)
+        def mask(g):
+            nc.scalar.activation(kept[g][:], away[g][:], ACT.Relu, bias=1.0, scale=-1.0)
 
         def take_old(g):
             lo, hi = TURNED[g]
             for j in range(0, hi - lo, P):
                 nc.scalar.activation(
-                    old_t[g][:, j : j + P], banks[g][:, j : j + P], ACT.Copy, scale=kept[g][:, j // P : j // P + 1]
+                    old_t[g][:, j : j + P], mem_banks[g][:, j : j + P], ACT.Copy, scale=kept[g][:, j // P : j // P + 1]
                 )
 
         def turn_back(g, tile, first):
             lo, hi = TURNED[g]
             for j in range(0, hi - lo, P):
                 nc.tensor.matmul(
-                    banks[4 + g][:, j : j + P],
+                    sum_banks[g][:, j : j + P],
                     lhsT=tile[:, j : j + P],
                     rhs=ident[:],
                     is_transpose=True,
@@ -163,23 +163,21 @@ def tile_picked_wkvput_tanh_l_kernel(tc, x_words, x_scales, mem, w1, slot, out):
 
         def leave(g):
             lo, hi = TURNED[g]
-            nc.scalar.copy(window[:, lo:hi], banks[4 + g][:, : hi - lo])
+            nc.scalar.copy(window[:, lo:hi], sum_banks[g][:, : hi - lo])
             nc.scalar.dma_start(out=out[:, lo:hi], in_=window[:, lo:hi])
 
         for g in groups:
-            turn(g, window, 0)
-        for g in groups:
-            turn(g, side, HALF)
-        sign(0)
+            turn(g, side, side_banks[g])
+        measure(0)
         take_new(0)
-        square(0)
-        sign(1)
-        flip(0)
-        square(1)
-        take_old(0)
-        flip(1)
+        measure(1)
+        mask(0)
+        mask(1)
         take_new(1)
-        take_old(1)
+        for g in groups:
+            turn(g, window, mem_banks[g])
+        for g in groups:
+            take_old(g)
         clear(*DIRECT[0])
         for i in range(len(DIRECT)):
             if i + 1 < len(DIRECT):

@@ -21,13 +21,14 @@ P = 128
 PACK = 4
 BANK = 512
 WORD_LOADS = ((0, 256), (256, 1024))
-PASSES = ((0, 128), (128, 256), (256, 512), (640, 896), (512, 640), (896, 1024))
+PASSES = ((0, 128), (128, 256), (256, 512), (512, 640), (640, 896), (896, 1024))
 FIRST = (0, 128)
 OVER_MEM = (128, 640)
 BY_SCALAR = (640, 1024)
 HALVES = ((0, 64), (64, 128))
-DIRECT = ((0, 128), (128, 384), (384, 640), (640, 896), (896, 1152), (1152, 1408))
-TURNED = ((1408, 1664), (1664, 2048))
+MEM_CUT = 768
+DIRECT = ((0, 256), (256, 768), (768, 1152), (1152, 1408))
+TURNED = ((1408, 1792), (1792, 2048))
 SHIFT = 2.0**-100
 FILLER = 2.0**-126
 
@@ -58,12 +59,13 @@ def tile_picked_wkvput_tanh_l_kernel(tc, x_words, x_scales, mem, w1, slot, out):
         nc.sync.dma_start(out=w_raw[:], in_=w1.rearrange("(p j) m -> p j m", j=PACK))
         load_scales(nc.scalar, 0)
         load_scales(nc.scalar, 1)
-        load_words(nc.gpsimd, 1)
         load_words(nc.sync, 0)
         load_scales(nc.sync, 2)
         load_scales(nc.sync, 3)
         nc.sync.dma_start(offsets[:], slot)
-        nc.sync.dma_start(out=window[:], in_=mem)
+        nc.sync.dma_start(out=window[:, :MEM_CUT], in_=mem[:, :MEM_CUT])
+        load_words(nc.sync, 1)
+        nc.sync.dma_start(out=window[:, MEM_CUT:], in_=mem[:, MEM_CUT:])
 
         nc.vector.memset(side[:, : U // 2], FILLER)
         nc.vector.memset(shift[:], SHIFT)

@@ -62,9 +62,9 @@ def tile_picked_wkvput_tanh_l_kernel(tc, x_words, x_scales, mem, w1, slot, out):
         load_words(nc.sync, 0)
         load_scales(nc.sync, 2)
         load_scales(nc.sync, 3)
-        nc.sync.dma_start(offsets[:], slot)
-        nc.sync.dma_start(out=window[:, :MEM_CUT], in_=mem[:, :MEM_CUT])
         load_words(nc.sync, 1)
+        nc.sync.dma_start(out=window[:, :MEM_CUT], in_=mem[:, :MEM_CUT])
+        nc.sync.dma_start(offsets[:], slot)
         nc.sync.dma_start(out=window[:, MEM_CUT:], in_=mem[:, MEM_CUT:])
 
         nc.vector.memset(side[:, : U // 2], FILLER)

@@ -26,7 +26,7 @@ FIRST = (0, 128)
 OVER_MEM = (128, 640)
 BY_SCALAR = (640, 1024)
 HALVES = ((0, 64), (64, 128))
-MEM_CUT = 768
+MEM_CUT = 1024
 DIRECT = ((0, 256), (256, 768), (768, 1152), (1152, 1408))
 TURNED = ((1408, 1792), (1792, 2048))
 SHIFT = 2.0**-100

@@ -27,8 +27,8 @@ OVER_MEM = (128, 640)
 BY_SCALAR = (640, 1024)
 HALVES = ((0, 64), (64, 128))
 MEM_CUT = 1024
-DIRECT = ((0, 256), (256, 768), (768, 1152), (1152, 1408))
-TURNED = ((1408, 1792), (1792, 2048))
+DIRECT = ((0, 128), (128, 256), (256, 448), (448, 640), (640, 832), (832, 1024), (1024, 1216), (1216, 1408))
+TURNED = ((1408, 1664), (1664, 2048))
 SHIFT = 2.0**-100
 FILLER = 2.0**-126
 
@@ -119,7 +119,6 @@ def tile_picked_wkvput_tanh_l_kernel(tc, x_words, x_scales, mem, w1, slot, out):
 
         def add(lo, hi):
             nc.vector.tensor_tensor(window[:, lo:hi], side[:, lo:hi], window[:, lo:hi], ALU.add)
-            nc.sync.dma_start(out=out[:, lo:hi], in_=window[:, lo:hi])
 
         groups = range(len(TURNED))
         new_t = [keep.tile([P, hi - lo], F32, align_bytes=256, name=f"new{lo}") for lo, hi in TURNED]
@@ -178,14 +177,15 @@ def tile_picked_wkvput_tanh_l_kernel(tc, x_words, x_scales, mem, w1, slot, out):
         take_new(1)
         for g in groups:
             turn(g, window, mem_banks[g])
-        for g in groups:
             take_old(g)
+            turn_back(g, new_t[g], True)
+            turn_back(g, old_t[g], False)
+            leave(g)
         clear(*DIRECT[0])
         for i in range(len(DIRECT)):
             if i + 1 < len(DIRECT):
                 clear(*DIRECT[i + 1])
             add(*DIRECT[i])
-        for g in groups:
-            turn_back(g, new_t[g], True)
-            turn_back(g, old_t[g], False)
-            leave(g)
+            if i % 2 == 1:
+                lo, hi = DIRECT[i - 1][0], DIRECT[i][1]
+                nc.sync.dma_start(out=out[:, lo:hi], in_=window[:, lo:hi])

@@ -27,8 +27,8 @@ OVER_MEM = (128, 640)
 BY_SCALAR = (640, 1024)
 HALVES = ((0, 64), (64, 128))
 MEM_CUT = 1024
-DIRECT = ((0, 128), (128, 256), (256, 448), (448, 640), (640, 832), (832, 1024), (1024, 1216), (1216, 1408))
-TURNED = ((1408, 1664), (1664, 2048))
+DIRECT = ((0, 192), (192, 384), (384, 576), (576, 768), (768, 1024), (1024, 1216), (1216, 1408), (1408, 1536))
+TURNED = ((1536, 1792), (1792, 2048))
 SHIFT = 2.0**-100
 FILLER = 2.0**-126
 

@@ -27,7 +27,7 @@ OVER_MEM = (128, 640)
 BY_SCALAR = (640, 1024)
 HALVES = ((0, 64), (64, 128))
 MEM_CUT = 1024
-DIRECT = ((0, 192), (192, 384), (384, 576), (576, 768), (768, 1024), (1024, 1216), (1216, 1408), (1408, 1536))
+DIRECT = ((0, 224, 448), (448, 640, 832), (832, 1056, 1280), (1280, 1408, 1536))
 TURNED = ((1536, 1792), (1792, 2048))
 SHIFT = 2.0**-100
 FILLER = 2.0**-126
@@ -123,8 +123,9 @@ def tile_picked_wkvput_tanh_l_kernel(tc, x_words, x_scales, mem, w1, slot, out):
         groups = range(len(TURNED))
         new_t = [keep.tile([P, hi - lo], F32, align_bytes=256, name=f"new{lo}") for lo, hi in TURNED]
         old_t = [keep.tile([P, hi - lo], F32, align_bytes=256, name=f"old{lo}") for lo, hi in TURNED]
-        away = [keep.tile([P, (hi - lo) // P], F32, align_bytes=32, name=f"away{lo}") for lo, hi in TURNED]
-        kept = [keep.tile([P, (hi - lo) // P], F32, align_bytes=32, name=f"kept{lo}") for lo, hi in TURNED]
+        first_block = [(lo - TURNED[0][0]) // P for lo, hi in TURNED]
+        away = keep.tile([P, (U - TURNED[0][0]) // P], F32, align_bytes=32)
+        kept = keep.tile([P, (U - TURNED[0][0]) // P], F32, align_bytes=32)
         side_banks, mem_banks, sum_banks = banks[6:8], banks[0:2], banks[2:4]
 
         def turn(g, tile, bank):
@@ -134,21 +135,18 @@ def tile_picked_wkvput_tanh_l_kernel(tc, x_words, x_scales, mem, w1, slot, out):
 
         def measure(g):
             lo, hi = TURNED[g]
-            nc.scalar.activation(away[g][:], side_banks[g][:, : hi - lo : P], ACT.Abs, bias=-1.0, scale=1.0 / FILLER)
+            blocks = away[:, first_block[g] : first_block[g] + (hi - lo) // P]
+            nc.scalar.activation(blocks, side_banks[g][:, : hi - lo : P], ACT.Abs, bias=-1.0, scale=1.0 / FILLER)
 
         def take_new(g):
             lo, hi = TURNED[g]
             nc.scalar.activation(new_t[g][:], side_banks[g][:, : hi - lo], ACT.Copy)
 
-        def mask(g):
-            nc.scalar.activation(kept[g][:], away[g][:], ACT.Relu, bias=1.0, scale=-1.0)
-
         def take_old(g):
             lo, hi = TURNED[g]
             for j in range(0, hi - lo, P):
-                nc.scalar.activation(
-                    old_t[g][:, j : j + P], mem_banks[g][:, j : j + P], ACT.Copy, scale=kept[g][:, j // P : j // P + 1]
-                )
+                b = first_block[g] + j // P
+                nc.scalar.activation(old_t[g][:, j : j + P], mem_banks[g][:, j : j + P], ACT.Copy, scale=kept[:, b : b + 1])
 
         def turn_back(g, tile, first):
             lo, hi = TURNED[g]
@@ -169,23 +167,21 @@ def tile_picked_wkvput_tanh_l_kernel(tc, x_words, x_scales, mem, w1, slot, out):
 
         for g in groups:
             turn(g, side, side_banks[g])
-        measure(0)
-        take_new(0)
-        measure(1)
-        mask(0)
-        mask(1)
-        take_new(1)
+        for g in groups:
+            measure(g)
+            take_new(g)
+        nc.scalar.activation(kept[:], away[:], ACT.Relu, bias=1.0, scale=-1.0)
         for g in groups:
             turn(g, window, mem_banks[g])
             take_old(g)
+        for g in groups:
             turn_back(g, new_t[g], True)
+        for g in groups:
             turn_back(g, old_t[g], False)
             leave(g)
-        clear(*DIRECT[0])
-        for i in range(len(DIRECT)):
-            if i + 1 < len(DIRECT):
-                clear(*DIRECT[i + 1])
-            add(*DIRECT[i])
-            if i % 2 == 1:
-                lo, hi = DIRECT[i - 1][0], DIRECT[i][1]
-                nc.sync.dma_start(out=out[:, lo:hi], in_=window[:, lo:hi])
+        for lo, mid, hi in DIRECT:
+            clear(lo, mid)
+            clear(mid, hi)
+            add(lo, mid)
+            add(mid, hi)
+            nc.sync.dma_start(out=out[:, lo:hi], in_=window[:, lo:hi])

@@ -59,8 +59,8 @@ def tile_picked_wkvput_tanh_l_kernel(tc, x_words, x_scales, mem, w1, slot, out):
         nc.sync.dma_start(out=w_raw[:], in_=w1.rearrange("(p j) m -> p j m", j=PACK))
         load_scales(nc.scalar, 0)
         load_scales(nc.scalar, 1)
+        load_scales(nc.scalar, 2)
         load_words(nc.sync, 0)
-        load_scales(nc.sync, 2)
         load_scales(nc.sync, 3)
         load_words(nc.sync, 1)
         nc.sync.dma_start(out=window[:, :MEM_CUT], in_=mem[:, :MEM_CUT])

@@ -20,14 +20,14 @@ ALU = mybir.AluOpType
 P = 128
 PACK = 4
 BANK = 512
-WORD_LOADS = ((0, 256), (256, 1024))
+WORD_LOADS = ((0, 1024),)
 PASSES = ((0, 128), (128, 256), (256, 512), (512, 640), (640, 896), (896, 1024))
 FIRST = (0, 128)
 OVER_MEM = (128, 640)
 BY_SCALAR = (640, 1024)
 HALVES = ((0, 64), (64, 128))
-MEM_CUT = 1024
 DIRECT = ((0, 224, 448), (448, 640, 832), (832, 1056, 1280), (1280, 1408, 1536))
+LATE = 832
 TURNED = ((1536, 1792), (1792, 2048))
 SHIFT = 2.0**-100
 FILLER = 2.0**-126
@@ -62,10 +62,8 @@ def tile_picked_wkvput_tanh_l_kernel(tc, x_words, x_scales, mem, w1, slot, out):
         load_scales(nc.scalar, 2)
         load_words(nc.sync, 0)
         load_scales(nc.sync, 3)
-        load_words(nc.sync, 1)
-        nc.sync.dma_start(out=window[:, :MEM_CUT], in_=mem[:, :MEM_CUT])
         nc.sync.dma_start(offsets[:], slot)
-        nc.sync.dma_start(out=window[:, MEM_CUT:], in_=mem[:, MEM_CUT:])
+        nc.sync.dma_start(out=window[:], in_=mem)
 
         nc.vector.memset(side[:, : U // 2], FILLER)
         nc.vector.memset(shift[:], SHIFT)
@@ -179,9 +177,14 @@ def tile_picked_wkvput_tanh_l_kernel(tc, x_words, x_scales, mem, w1, slot, out):
         for g in groups:
             turn_back(g, old_t[g], False)
             leave(g)
+        def store(lo, hi):
+            nc.sync.dma_start(out=out[:, lo:hi], in_=window[:, lo:hi])
+
         for lo, mid, hi in DIRECT:
             clear(lo, mid)
             clear(mid, hi)
             add(lo, mid)
+            if lo >= LATE:
+                store(lo, mid)
             add(mid, hi)
-            nc.sync.dma_start(out=out[:, lo:hi], in_=window[:, lo:hi])
+            store(mid if lo >= LATE else lo, hi)

@@ -22,8 +22,8 @@ PACK = 4
 BANK = 512
 WORD_LOADS = ((0, 1024),)
 PASSES = ((0, 128), (128, 256), (256, 512), (512, 640), (640, 896), (896, 1024))
-FIRST = (0, 128)
-OVER_MEM = (128, 640)
+FIRST = (0, 160)
+OVER_MEM = (160, 640)
 BY_SCALAR = (640, 1024)
 HALVES = ((0, 64), (64, 128))
 DIRECT = ((0, 224, 448), (448, 640, 832), (832, 1056, 1280), (1280, 1408, 1536))

from contextlib import ExitStack

import concourse.mybir as mybir
from concourse.masks import make_identity

K, T, M, U = 512, 1024, 128, 2048
FLOPS = 2 * K * M * T

F32 = mybir.dt.float32
BF16 = mybir.dt.bfloat16
I32 = mybir.dt.int32
U32 = mybir.dt.uint32
U16 = mybir.dt.uint16
U8 = mybir.dt.uint8
FP8X4 = mybir.dt.float8_e4m3fn_x4
FP4X4 = mybir.dt.float4_e2m1fn_x4
ACT = mybir.ActivationFunctionType
ALU = mybir.AluOpType

P = 128
PACK = 4
BANK = 512
WORD_LOADS = ((0, 1024),)
PASSES = ((0, 128), (128, 256), (256, 512), (512, 640), (640, 896), (896, 1024))
FIRST = (0, 160)
OVER_MEM = (160, 640)
BY_SCALAR = (640, 1024)
HALVES = ((0, 64), (64, 128))
DIRECT = ((0, 224, 448), (448, 640, 832), (832, 1056, 1280), (1280, 1408, 1536))
LATE = 832
TURNED = ((1536, 1792), (1792, 2048))
SHIFT = 2.0**-100
FILLER = 2.0**-126


def tile_picked_wkvput_tanh_l_kernel(tc, x_words, x_scales, mem, w1, slot, out):
    nc = tc.nc
    with ExitStack() as ctx:
        keep = ctx.enter_context(tc.tile_pool(name="keep", bufs=1))
        psum = ctx.enter_context(tc.psum_pool(name="psum", bufs=1))

        offsets = keep.tile([P, T // 16], U16, align_bytes=256)
        w_raw = keep.tile([P, PACK, M], F32, align_bytes=256)
        x_tiles = [keep.tile([P, 2 * (hi - lo)], U8, align_bytes=256, name=f"x{lo}") for lo, hi in WORD_LOADS]
        plane = keep.tile([P, T], U8, align_bytes=256)
        window = keep.tile([P, U], F32, align_bytes=256)
        side = keep.tile([P, U], F32, align_bytes=256)
        shift = keep.tile([P, FIRST[1] - FIRST[0]], F32, align_bytes=256)
        ident = keep.tile([P, P], F32, align_bytes=256)
        banks = [psum.tile([P, BANK], F32, name=f"bank{b}") for b in range(8)]

        def load_scales(queue, q):
            queue.dma_start(out=plane[q:P:32, :].bitcast(I32), in_=x_scales[0, q:16:4, :].bitcast(I32))

        def load_words(queue, i):
            lo, hi = WORD_LOADS[i]
            queue.dma_start(out=x_tiles[i][:].bitcast(I32), in_=x_words[0, :, 2 * lo : 2 * hi].bitcast(I32))

        nc.sync.dma_start(out=w_raw[:], in_=w1.rearrange("(p j) m -> p j m", j=PACK))
        load_scales(nc.scalar, 0)
        load_scales(nc.scalar, 1)
        load_scales(nc.scalar, 2)
        load_words(nc.sync, 0)
        load_scales(nc.sync, 3)
        nc.sync.dma_start(offsets[:], slot)
        nc.sync.dma_start(out=window[:], in_=mem)

        nc.vector.memset(side[:, : U // 2], FILLER)
        nc.vector.memset(shift[:], SHIFT)
        nc.scalar.activation(side[:, U // 2 :], side[:, : U // 2], ACT.Copy)
        make_identity(nc, ident[:])

        w_grouped = keep.tile([P, M, PACK], BF16, align_bytes=64)
        w_codes = keep.tile([P, M], U32, align_bytes=64)
        w_plane = keep.tile([P, M], U8, align_bytes=64)
        for lo, hi in HALVES:
            nc.vector.tensor_copy(
                out=w_grouped[:, lo:hi, :].rearrange("p (c i) j -> p c j i", i=4),
                in_=w_raw[:, :, lo:hi].rearrange("p j (c i) -> p c j i", i=4),
            )
        for lo, hi in HALVES:
            nc.vector.quantize_mx(
                out=w_codes[:, lo:hi].bitcast(FP8X4),
                scales=w_plane[:, lo:hi],
                in_=w_grouped[:, lo:hi, :].rearrange("p m j -> p (m j)"),
            )

        y = keep.tile([P, T], F32, align_bytes=256)
        for i, (lo, hi) in enumerate(PASSES):
            tile, base = [(t, a) for t, (a, b) in zip(x_tiles, WORD_LOADS) if a <= lo and hi <= b][0]
            acc = banks[i][:, : hi - lo]
            nc.tensor.matmul_mx(
                out=acc,
                lhsT=w_codes[:].bitcast(FP8X4),
                lhsT_scale=w_plane[:],
                rhs=tile[:, 2 * (lo - base) : 2 * (hi - base)].bitcast(FP4X4),
                rhs_scale=plane[:, lo:hi],
                start=True,
                stop=True,
            )
            if lo >= BY_SCALAR[0]:
                nc.scalar.activation(y[:, lo:hi], acc, ACT.Tanh, bias=SHIFT)
            else:
                nc.scalar.activation(y[:, lo:hi], acc, ACT.Tanh)

        def picks(piece):
            return offsets[:, piece[0] // 16 : piece[1] // 16]

        nc.vector.tensor_tensor(side[:].indirect(picks(FIRST)), y[:, FIRST[0] : FIRST[1]], shift[:], ALU.add)
        nc.vector.tensor_copy(window[:].indirect(picks(OVER_MEM)), y[:, OVER_MEM[0] : OVER_MEM[1]])
        nc.scalar.activation(side[:].indirect(picks(BY_SCALAR)), y[:, BY_SCALAR[0] : BY_SCALAR[1]], ACT.Copy)

        def clear(lo, hi):
            nc.vector.scalar_tensor_tensor(
                window[:, lo:hi], side[:, lo:hi], FILLER, window[:, lo:hi], ALU.is_equal, ALU.mult
            )

        def add(lo, hi):
            nc.vector.tensor_tensor(window[:, lo:hi], side[:, lo:hi], window[:, lo:hi], ALU.add)

        groups = range(len(TURNED))
        new_t = [keep.tile([P, hi - lo], F32, align_bytes=256, name=f"new{lo}") for lo, hi in TURNED]
        old_t = [keep.tile([P, hi - lo], F32, align_bytes=256, name=f"old{lo}") for lo, hi in TURNED]
        first_block = [(lo - TURNED[0][0]) // P for lo, hi in TURNED]
        away = keep.tile([P, (U - TURNED[0][0]) // P], F32, align_bytes=32)
        kept = keep.tile([P, (U - TURNED[0][0]) // P], F32, align_bytes=32)
        side_banks, mem_banks, sum_banks = banks[6:8], banks[0:2], banks[2:4]

        def turn(g, tile, bank):
            lo, hi = TURNED[g]
            for c in range(lo, hi, P):
                nc.tensor.transpose(bank[:, c - lo : c - lo + P], tile[:, c : c + P], ident[:])

        def measure(g):
            lo, hi = TURNED[g]
            blocks = away[:, first_block[g] : first_block[g] + (hi - lo) // P]
            nc.scalar.activation(blocks, side_banks[g][:, : hi - lo : P], ACT.Abs, bias=-1.0, scale=1.0 / FILLER)

        def take_new(g):
            lo, hi = TURNED[g]
            nc.scalar.activation(new_t[g][:], side_banks[g][:, : hi - lo], ACT.Copy)

        def take_old(g):
            lo, hi = TURNED[g]
            for j in range(0, hi - lo, P):
                b = first_block[g] + j // P
                nc.scalar.activation(old_t[g][:, j : j + P], mem_banks[g][:, j : j + P], ACT.Copy, scale=kept[:, b : b + 1])

        def turn_back(g, tile, first):
            lo, hi = TURNED[g]
            for j in range(0, hi - lo, P):
                nc.tensor.matmul(
                    sum_banks[g][:, j : j + P],
                    lhsT=tile[:, j : j + P],
                    rhs=ident[:],
                    is_transpose=True,
                    start=(first and j == 0),
                    stop=(not first and lo + j + P == hi),
                )

        def leave(g):
            lo, hi = TURNED[g]
            nc.scalar.copy(window[:, lo:hi], sum_banks[g][:, : hi - lo])
            nc.scalar.dma_start(out=out[:, lo:hi], in_=window[:, lo:hi])

        for g in groups:
            turn(g, side, side_banks[g])
        for g in groups:
            measure(g)
            take_new(g)
        nc.scalar.activation(kept[:], away[:], ACT.Relu, bias=1.0, scale=-1.0)
        for g in groups:
            turn(g, window, mem_banks[g])
            take_old(g)
        for g in groups:
            turn_back(g, new_t[g], True)
        for g in groups:
            turn_back(g, old_t[g], False)
            leave(g)
        def store(lo, hi):
            nc.sync.dma_start(out=out[:, lo:hi], in_=window[:, lo:hi])

        for lo, mid, hi in DIRECT:
            clear(lo, mid)
            clear(mid, hi)
            add(lo, mid)
            if lo >= LATE:
                store(lo, mid)
            add(mid, hi)
            store(mid if lo >= LATE else lo, hi)
